import numpy as np
import ml_dtypes


def mxq(x, axis, fmt="e4m3"):
    dtype, down = {"e4m3": (ml_dtypes.float8_e4m3fn, 7), "e5m2": (ml_dtypes.float8_e5m2, 14)}[fmt]
    v = np.moveaxis(np.asarray(x, np.float32).astype(ml_dtypes.bfloat16).astype(np.float64), axis, -1)
    blocks = v.reshape(v.shape[:-1] + (-1, 32))
    amax = np.abs(blocks).max(-1, keepdims=True)
    byte = np.maximum(np.where(amax > 0, np.frexp(amax)[1] - 1 + 127, 0) - down, 1)
    scale = np.exp2(byte - 127.0)
    codes = (blocks / scale).astype(np.float32).astype(dtype).astype(np.float64)
    return np.moveaxis((codes * scale).reshape(v.shape), -1, axis)


WIDE = False


def mx_kscale(k):
    if not WIDE:
        return np.ones(k)
    levels = np.array([10, -10, 5, -5, 0])
    if k % 512:
        return np.exp2(np.random.permutation(np.resize(levels, k // 32))).repeat(32)
    a = np.empty((k // 512, 16))
    for p in range(k // 512):
        a[p, :8] = np.random.permutation(np.resize(levels, 8))
        for g in range(8):
            far = levels[np.abs(levels - a[p, g]) >= 10]
            a[p, g + 8] = far[np.random.randint(len(far))]
    return np.exp2(a.ravel()).repeat(32)


def f64(x):
    return np.asarray(x).astype(np.float64)


def striped(idx):
    return np.tile(np.asarray(idx).reshape(-1, 16).T, (8, 1)).astype(np.uint16)


def unstriped(offs):
    return offs[:16].T.reshape(-1).astype(np.int64)


def striped8(idx):
    return np.asarray(idx).reshape(8, -1, 16).transpose(0, 2, 1).reshape(128, -1).astype(np.uint16)


def unstriped8(offs):
    return offs.reshape(8, 16, -1).transpose(0, 2, 1).reshape(8, -1).astype(np.int64)


def pick8(x, idx, run):
    r = np.arange(len(x))
    return x[r[:, None], idx[r % (8 * run) // run]]


E2M1 = np.array([0.0, 0.5, 1.0, 1.5, 2.0, 3.0, 4.0, 6.0, -0.0, -0.5, -1.0, -1.5, -2.0, -3.0, -4.0, -6.0])


def pack_weight(w, fmt):
    k, n = w.shape
    w = f64(np.asarray(w, np.float32).astype(ml_dtypes.bfloat16)).reshape(k // 32, 32, n)
    amax = np.abs(w).max(1)
    if fmt == "e4m3":
        byte = np.frexp(amax)[1] - 1 + 127 - 7
    else:
        mant, ex = np.frexp(amax / 6.0)
        byte = np.where(mant > 0.5, ex, ex - 1) + 127
    byte = np.clip(np.where(amax > 0, byte, 1), 1, 254)
    scaled = (w * np.exp2(127.0 - byte)[:, None, :]).reshape(k, n).astype(np.float32)
    by_word = np.ascontiguousarray(scaled.reshape(k // 512, 128, 4, n).transpose(0, 1, 3, 2))
    if fmt == "e4m3":
        words = by_word.astype(ml_dtypes.float8_e4m3fn).view(np.uint8)
    else:
        c = by_word.astype(ml_dtypes.float4_e2m1fn).view(np.uint8) & 0xF
        words = (c[..., 0::2] | (c[..., 1::2] << 4)).reshape(k // 512, 128, 2 * n)
    return np.ascontiguousarray(words), np.ascontiguousarray(byte.astype(np.uint8).reshape(k // 512, 16, n))


def unpack_weight(words, scales, fmt):
    g, _, n = scales.shape
    words = np.ascontiguousarray(words).reshape(g, 128, n, -1)
    if fmt == "e4m3":
        vals = words.view(ml_dtypes.float8_e4m3fn).astype(np.float64)
    else:
        nib = np.empty((g, 128, n, 4), np.uint8)
        nib[..., 0::2] = words & 0xF
        nib[..., 1::2] = words >> 4
        vals = E2M1[nib]
    vals = vals * np.repeat(np.exp2(scales.astype(np.float64) - 127.0), 8, axis=1)[..., None]
    return vals.transpose(0, 1, 3, 2).reshape(g * 512, n)


def sgn(shape):
    return np.random.uniform(0.5, 2.0, shape) * np.where(np.random.standard_normal(shape) < 0, -1.0, 1.0)


K, J, R, T, F, Z, M, S, O, N, E = 512, 512, 512, 2048, 2048, 512, 1024, 256, 128, 256, 256


def setup_inputs():
    n = np.random.standard_normal
    idx = np.random.permutation(T)[:J]
    idx2 = np.stack([np.random.permutation(F)[:R] for _ in range(8)])
    idx3 = np.random.permutation(M)[:J]
    idx4 = np.stack([np.random.permutation(J)[:S] for _ in range(8)])
    idx5 = np.random.permutation(J)[:S]
    idx6 = np.stack([np.random.permutation(E)[:O] for _ in range(8)])
    idx7 = np.stack([np.random.permutation(E)[:O] for _ in range(8)])
    fk = mx_kscale(K)
    fz = mx_kscale(Z)
    fr = mx_kscale(R)
    xtp = pack_weight(n((K, T)) * fk[:, None], "e4m3")
    xop = pack_weight(n((Z, M)) / fz[:, None], "e2m1")
    w2p = pack_weight(n((Z, R)) * 1 / np.sqrt(Z) * fz[:, None], "e4m3")
    wbp = pack_weight(n((R, N)) * 1 / np.sqrt(R) / fr[:, None], "e4m3")
    return {
        "xt_words": xtp[0],
        "xt_scales": xtp[1],
        "ua": (np.random.randint(-7, 8, (K, F)).astype(np.float64)).astype(np.float32),
        "ha": ((np.random.randint(8, 25, (K, 1)) / 1024.0) / fk[:, None]).astype(np.float32),
        "xo_words": xop[0],
        "xo_scales": xop[1],
        "w2_words": w2p[0],
        "w2_scales": w2p[1],
        "sa": (sgn((R, 1)) * fr[:, None]).astype(np.float32),
        "sb": (sgn((R, 1)) * fr[:, None]).astype(np.float32),
        "wb_words": wbp[0],
        "wb_scales": wbp[1],
        "tz": (np.random.randint(-7, 8, (N, E)).astype(np.float64)).astype(np.float32),
        "so": (np.random.randint(8, 25, (N, 1)) / 64.0).astype(np.float32),
        "sp": (np.random.randint(4, 15, (N, 1)) / 64.0).astype(np.float32),
        "offs": striped(idx),
        "offs2": striped8(idx2),
        "offs3": striped(idx3),
        "offs4": striped8(idx4),
        "offs5": striped(idx5),
        "offs6": striped8(idx6),
        "offs7": striped8(idx7),
    }


def reference(xt_words, xt_scales, ua, ha, xo_words, xo_scales, w2_words, w2_scales, sa, sb, wb_words, wb_scales, tz, so, sp, offs, offs2, offs3, offs4, offs5, offs6, offs7):
    idx = unstriped(offs)
    idx2 = unstriped8(offs2)
    idx3 = unstriped(offs3)
    idx4 = unstriped8(offs4)
    idx5 = unstriped(offs5)
    idx6 = unstriped8(offs6)
    idx7 = unstriped8(offs7)
    xtu = unpack_weight(xt_words, xt_scales, "e4m3")
    xou = unpack_weight(xo_words, xo_scales, "e2m1")
    w2u = unpack_weight(w2_words, w2_scales, "e4m3")
    wbu = unpack_weight(wb_words, wb_scales, "e4m3")
    wc = pick8(f64(ua), idx2, 64) * f64(ha)
    wcq = mxq(wc, 0, "e4m3")
    xtidxg = xtu[:, idx]
    xoidx3g = xou[:, idx3]
    a = wcq.T @ xtidxg + w2u.T @ xoidx3g
    h1 = np.maximum(pick8(a, idx4, 64) * f64(sa), a[:, idx5] * f64(sb))
    hid = h1.reshape(R, O, S // O).max(axis=2)
    hidq = mxq(hid, 0, "e4m3")
    p = wbu.T @ hidq
    y = np.maximum(np.minimum(p, pick8(f64(tz), idx6, 16) * f64(so)), pick8(f64(tz), idx7, 16) * f64(sp))
    return y

@@ -1,0 +1,248 @@
+from contextlib import ExitStack
+
+import concourse.mybir as mybir
+
+F32 = mybir.dt.float32
+BF16 = mybir.dt.bfloat16
+I32 = mybir.dt.int32
+U32 = mybir.dt.uint32
+U16 = mybir.dt.uint16
+U8 = mybir.dt.uint8
+FP8X4 = mybir.dt.float8_e4m3fn_x4
+FP4X4 = mybir.dt.float4_e2m1fn_x4
+COPY = mybir.ActivationFunctionType.Copy
+MAX = mybir.AluOpType.max
+MIN = mybir.AluOpType.min
+XY = mybir.AxisListType.XY
+
+P = 128
+PACK = 4
+QUADS = 4
+K, J, R, T, F, Z, M, S, O, N, E = 512, 512, 512, 2048, 2048, 512, 1024, 256, 128, 256, 256
+NB = N // P
+HALF = J // 2
+XT_ROW = 4
+
+FLOPS = 2 * K * R * J + 2 * Z * R * J + 2 * R * N * O
+
+
+def tile_picked_tokens_codes_bank_pooledgroups_one_lastbounds_kernel(
+    tc, xt_words, xt_scales, ua, ha, xo_words, xo_scales, w2_words, w2_scales, sa, sb,
+    wb_words, wb_scales, tz, so, sp, offs, offs2, offs3, offs4, offs5, offs6, offs7, out,
+):
+    nc = tc.nc
+    with ExitStack() as ctx:
+        keep = ctx.enter_context(tc.tile_pool(name="keep", bufs=1))
+        psum = ctx.enter_context(tc.psum_pool(name="psum", bufs=1))
+
+        def load_list(src, name):
+            lst = keep.tile(list(src.shape), U16, name=name)
+            nc.sync.dma_start(lst[:], src)
+            return lst
+
+        def zeroed_bytes(width, name):
+            t = keep.tile([P, width], U8, name=name, align_bytes=64)
+            nc.vector.memset(t[:].bitcast(I32), 0)
+            return t
+
+        xt_scale_rows = zeroed_bytes(T, "xt_scale_rows")
+        xo_scale_rows = zeroed_bytes(M, "xo_scale_rows")
+        w2_scale_rows = zeroed_bytes(R, "w2_scale_rows")
+        wb_plane = zeroed_bytes(N, "wb_plane")
+
+        def load_columns(queue, src, name):
+            t = keep.tile([P, PACK], F32, name=name)
+            queue.dma_start(t[:], src.rearrange("(p t) o -> p (t o)", t=PACK))
+            return t
+
+        def load_scale_rows(dst, src, first):
+            for q in range(QUADS):
+                nc.gpsimd.dma_start(
+                    dst[32 * q + first : 32 * q + first + 4, :].bitcast(I32),
+                    src[0, 4 * q : 4 * q + 4, :].bitcast(I32),
+                )
+
+        load_scale_rows(xt_scale_rows, xt_scales, XT_ROW)
+        sa_sb = load_columns(nc.gpsimd, sa, "sa_sb")
+        sb_sb = load_columns(nc.gpsimd, sb, "sb_sb")
+        wb_stage = keep.tile([4, QUADS, N // 4], I32, name="wb_stage")
+        nc.gpsimd.dma_start(wb_stage[:], wb_scales[0].rearrange("(q i) c -> i q c", i=4).bitcast(I32))
+        so_sb = keep.tile([P, NB], F32, name="so_sb")
+        sp_sb = keep.tile([P, NB], F32, name="sp_sb")
+        with nc.allow_non_contiguous_dma(reason="one value a partition and block"):
+            nc.gpsimd.dma_start(so_sb[:], so.rearrange("(b p) o -> p (b o)", p=P))
+            nc.gpsimd.dma_start(sp_sb[:], sp.rearrange("(b p) o -> p (b o)", p=P))
+
+        ua_rows = ua.rearrange("(p t) f -> p t f", t=PACK)
+        ua_sb = [keep.tile([P, F], F32, name="ua%d" % t) for t in range(PACK)]
+        list2 = load_list(offs2, "list2")
+        ha_sb = load_columns(nc.sync, ha, "ha_sb")
+        xo_sb = keep.tile([P, M], U16, name="xo_sb")
+        nc.sync.dma_start(xo_sb[:].bitcast(I32), xo_words[0].bitcast(I32))
+        nc.sync.dma_start(ua_sb[0][:], ua_rows[:, 0, :])
+        xo_stage = keep.tile([P, 2, M // 4], I32, name="xo_stage")
+        for u in range(2):
+            nc.sync.dma_start(
+                xo_stage[64 * u : 64 * u + 4, :, :],
+                xo_scales[0, 8 * u : 8 * u + 8, :].rearrange("(q i) c -> i q c", i=4).bitcast(I32),
+            )
+        w2_stage = keep.tile([4, QUADS, R // 4], I32, name="w2_stage")
+        nc.sync.dma_start(w2_stage[:], w2_scales[0].rearrange("(q i) c -> i q c", i=4).bitcast(I32))
+        list3 = load_list(offs3, "list3")
+        nc.sync.dma_start(ua_sb[1][:], ua_rows[:, 1, :])
+        list1 = load_list(offs, "list1")
+        nc.sync.dma_start(ua_sb[2][:], ua_rows[:, 2, :])
+        nc.sync.dma_start(ua_sb[3][:], ua_rows[:, 3, :])
+        w2_sb = keep.tile([P, R], I32, name="w2_sb")
+        nc.sync.dma_start(w2_sb[:], w2_words[0].rearrange("p n t -> p (n t)").bitcast(I32))
+        xt_sb = keep.tile([P, T], I32, name="xt_sb")
+        nc.sync.dma_start(xt_sb[:], xt_words[0].rearrange("p n t -> p (n t)").bitcast(I32))
+        list4 = load_list(offs4, "list4")
+        list5 = load_list(offs5, "list5")
+        wb_sb = keep.tile([P, N], I32, name="wb_sb", align_bytes=64)
+        nc.sync.dma_start(wb_sb[:], wb_words[0].rearrange("p n t -> p (n t)").bitcast(I32))
+        tz_sb = [keep.tile([P, E], F32, name="tz%d" % b) for b in range(NB)]
+        for b in range(NB):
+            nc.sync.dma_start(tz_sb[b][:], tz[b * P : (b + 1) * P, :])
+        list6 = load_list(offs6, "list6")
+        list7 = load_list(offs7, "list7")
+
+        xo_codes = keep.tile([P, 2 * J], U8, name="xo_codes", align_bytes=64)
+        xo_plane = keep.tile([P, J], U8, name="xo_plane", align_bytes=64)
+        xt_plane = keep.tile([P, J], U8, name="xt_plane", align_bytes=64)
+        nc.vector.tensor_copy(xo_codes[:].bitcast(U16), xo_sb[:].indirect(list3[:]))
+        for q in range(QUADS):
+            first = 64 * (q // 2)
+            nc.vector.tensor_copy(
+                xo_scale_rows[:].bitcast(I32)[32 * q : 32 * q + 4, :], xo_stage[first : first + 4, q % 2, :]
+            )
+        nc.vector.tensor_copy(xo_plane[:], xo_scale_rows[:].indirect(list3[:]))
+
+        def spread(plane, stage):
+            words = plane[:].bitcast(I32)
+            for q in range(QUADS):
+                nc.vector.tensor_copy(words[32 * q : 32 * q + 4, :], stage[:, q, :])
+
+        spread(w2_scale_rows, w2_stage)
+        w2_plane = keep.tile([P, R], U8, name="w2_plane", align_bytes=64)
+        nc.vector.tensor_copy(
+            w2_plane[:].rearrange("p (m c) -> p m c", m=PACK),
+            w2_scale_rows[:].rearrange("p (c m) -> p m c", m=PACK),
+        )
+        nc.vector.tensor_copy(xt_plane[:], xt_scale_rows[:].indirect(list1[:]))
+        spread(wb_plane, wb_stage)
+
+        wc_rows = keep.tile([P, PACK, R], BF16, name="wc_rows")
+        for t in range(PACK):
+            nc.scalar.activation(
+                wc_rows[:, t, :], ua_sb[t][:].indirect(list2[:]), COPY, scale=ha_sb[:, t : t + 1]
+            )
+
+        w2_codes = keep.tile([P, R], I32, name="w2_codes", align_bytes=64)
+        nc.vector.tensor_copy(
+            w2_codes[:].rearrange("p (m g e) -> p g m e", m=PACK, e=4),
+            w2_sb[:].rearrange("p (g e m) -> p g m e", m=PACK, e=4),
+        )
+
+        a0_ps = [psum.tile([P, HALF], F32, name="a0_ps%d" % h) for h in range(2)]
+        a_ps = [psum.tile([P, J], F32, name="a_ps%d" % m) for m in range(1, PACK)]
+
+        def notes_pass(dst, m, lo, hi):
+            cols = slice(m * P, (m + 1) * P)
+            nc.tensor.matmul_mx(
+                out=dst, lhsT=w2_codes[:, cols].bitcast(FP8X4), lhsT_scale=w2_plane[:, cols],
+                rhs=xo_codes[:, 2 * lo : 2 * hi].bitcast(FP4X4), rhs_scale=xo_plane[:, lo:hi],
+                start=True, stop=False,
+            )
+
+        for h in range(2):
+            notes_pass(a0_ps[h][:], 0, h * HALF, (h + 1) * HALF)
+        for m in range(1, PACK):
+            notes_pass(a_ps[m - 1][:], m, 0, J)
+
+        wc_view = wc_rows[:].rearrange("p t (g e m) -> p g m e t", e=2, m=PACK)
+        wc_codes, wc_plane = [], []
+        for u in range(2):
+            woven = keep.tile([P, 2 * P * PACK], BF16, name="woven%d" % u, align_bytes=64)
+            dst = woven[:].rearrange("p (m g e t) -> p g m e t", m=2, e=2, t=PACK)
+            src = wc_view[:, :, 2 * u : 2 * u + 2, :, :]
+            if u == 0:
+                nc.vector.tensor_copy(dst, src)
+            else:
+                nc.scalar.copy(dst, src)
+            codes = keep.tile([P, 2 * P], U32, name="wc_codes%d" % u, align_bytes=64)
+            plane = keep.tile([P, 2 * P], U8, name="wc_plane%d" % u, align_bytes=64)
+            nc.vector.quantize_mx(out=codes[:].bitcast(FP8X4), scales=plane[:], in_=woven[:])
+            wc_codes.append(codes)
+            wc_plane.append(plane)
+
+        xt_codes = keep.tile([P, J], U32, name="xt_codes", align_bytes=64)
+        for h in range(2):
+            nc.vector.tensor_copy(
+                xt_codes[:, h * HALF : (h + 1) * HALF],
+                xt_sb[:].bitcast(U32).indirect(list1[:, h * HALF // 16 : (h + 1) * HALF // 16]),
+            )
+
+        def tokens_pass(dst, m, lo, hi):
+            cols = slice(m % 2 * P, (m % 2 + 1) * P)
+            nc.tensor.matmul_mx(
+                out=dst, lhsT=wc_codes[m // 2][:, cols].bitcast(FP8X4), lhsT_scale=wc_plane[m // 2][:, cols],
+                rhs=xt_codes[:, lo:hi].bitcast(FP8X4), rhs_scale=xt_plane[XT_ROW:, lo:hi],
+                start=False, stop=True,
+            )
+
+        a_sb = [keep.tile([P, J], F32, name="a_sb%d" % m) for m in range(PACK)]
+        for h in range(2):
+            tokens_pass(a0_ps[h][:], 0, h * HALF, (h + 1) * HALF)
+            nc.scalar.copy(a_sb[0][:, h * HALF : (h + 1) * HALF], a0_ps[h][:])
+        for m in range(1, PACK):
+            tokens_pass(a_ps[m - 1][:], m, 0, J)
+            nc.vector.tensor_copy(a_sb[m][:], a_ps[m - 1][:])
+
+        hid = keep.tile([P, O, PACK], BF16, name="hid", align_bytes=64)
+        for m in range(PACK):
+            parts = 2 if m == PACK - 1 else 1
+            width = S // parts
+            picked = keep.tile([P, parts, 2, width], F32, name="picked", tag="picked", bufs=2)
+            for h in range(parts):
+                cols = slice(h * width // 16, (h + 1) * width // 16)
+                nc.scalar.activation(
+                    picked[:, h, 0, :], a_sb[m][:].indirect(list4[:, cols]), COPY, scale=sa_sb[:, m : m + 1]
+                )
+                nc.scalar.activation(
+                    picked[:, h, 1, :], a_sb[m][:].indirect(list5[:, cols]), COPY, scale=sb_sb[:, m : m + 1]
+                )
+                nc.vector.tensor_reduce(
+                    hid[:, h * width // 2 : (h + 1) * width // 2, m],
+                    picked[:, h, :, :].rearrange("p w (o e) -> p o w e", e=2),
+                    XY, MAX,
+                )
+
+        bounds = keep.tile([P, 2, NB, O], F32, name="bounds", tag="picked", bufs=2)
+        for b in range(NB):
+            nc.scalar.activation(
+                bounds[:, 0, b, :], tz_sb[b][:].indirect(list6[:]), COPY, scale=so_sb[:, b : b + 1]
+            )
+        for b in range(NB):
+            nc.scalar.activation(
+                bounds[:, 1, b, :], tz_sb[b][:].indirect(list7[:]), COPY, scale=sp_sb[:, b : b + 1]
+            )
+
+        hid_codes = keep.tile([P, O], U32, name="hid_codes", align_bytes=64)
+        hid_plane = keep.tile([P, O], U8, name="hid_plane", align_bytes=64)
+        nc.vector.quantize_mx(
+            out=hid_codes[:].bitcast(FP8X4), scales=hid_plane[:], in_=hid[:].rearrange("p o m -> p (o m)")
+        )
+        capped = keep.tile([P, NB, O], F32, name="capped")
+        result = keep.tile([P, NB, O], F32, name="result")
+        for b in range(NB):
+            cols = slice(b * P, (b + 1) * P)
+            p_ps = psum.tile([P, O], F32, name="p_ps%d" % b)
+            nc.tensor.matmul_mx(
+                out=p_ps[:], lhsT=wb_sb[:, cols].bitcast(FP8X4), lhsT_scale=wb_plane[:, cols],
+                rhs=hid_codes[:].bitcast(FP8X4), rhs_scale=hid_plane[:], start=True, stop=True,
+            )
+            nc.vector.tensor_tensor(capped[:, b, :], p_ps[:], bounds[:, 0, b, :], MIN)
+        for b in range(NB):
+            nc.vector.tensor_tensor(result[:, b, :], capped[:, b, :], bounds[:, 1, b, :], MAX)
+        nc.sync.dma_start(out.rearrange("(b p) o -> p b o", p=P), result[:])

@@ -50,72 +50,86 @@ def tile_picked_tokens_codes_bank_pooledgroups_one_lastbounds_kernel(
         w2_scale_rows = zeroed_bytes(R, "w2_scale_rows")
         wb_plane = zeroed_bytes(N, "wb_plane")
 
-        def load_columns(queue, src, name):
+        def load_columns(src, name):
             t = keep.tile([P, PACK], F32, name=name)
-            queue.dma_start(t[:], src.rearrange("(p t) o -> p (t o)", t=PACK))
+            nc.sync.dma_start(t[:], src.rearrange("(p t) o -> p (t o)", t=PACK))
             return t
 
-        def load_scale_rows(dst, src, first):
-            for q in range(QUADS):
-                nc.gpsimd.dma_start(
-                    dst[32 * q + first : 32 * q + first + 4, :].bitcast(I32),
-                    src[0, 4 * q : 4 * q + 4, :].bitcast(I32),
-                )
+        def load_blocks(src, name):
+            t = keep.tile([P, NB], F32, name=name)
+            with nc.allow_non_contiguous_dma(reason="one value a partition and block"):
+                nc.sync.dma_start(t[:], src.rearrange("(b p) o -> p (b o)", p=P))
+            return t
 
-        load_scale_rows(xt_scale_rows, xt_scales, XT_ROW)
-        sa_sb = load_columns(nc.gpsimd, sa, "sa_sb")
-        sb_sb = load_columns(nc.gpsimd, sb, "sb_sb")
-        wb_stage = keep.tile([4, QUADS, N // 4], I32, name="wb_stage")
-        nc.gpsimd.dma_start(wb_stage[:], wb_scales[0].rearrange("(q i) c -> i q c", i=4).bitcast(I32))
-        so_sb = keep.tile([P, NB], F32, name="so_sb")
-        sp_sb = keep.tile([P, NB], F32, name="sp_sb")
-        with nc.allow_non_contiguous_dma(reason="one value a partition and block"):
-            nc.gpsimd.dma_start(so_sb[:], so.rearrange("(b p) o -> p (b o)", p=P))
-            nc.gpsimd.dma_start(sp_sb[:], sp.rearrange("(b p) o -> p (b o)", p=P))
+        def load_scale_half(stage, src, u):
+            nc.sync.dma_start(
+                stage[64 * u : 64 * u + 4, :, :],
+                src[0, 8 * u : 8 * u + 8, :].rearrange("(q i) c -> i q c", i=4).bitcast(I32),
+            )
+
+        def load_scale_whole(src, width, name):
+            stage = keep.tile([4, QUADS, width // 4], I32, name=name)
+            nc.sync.dma_start(stage[:], src[0].rearrange("(q i) c -> i q c", i=4).bitcast(I32))
+            return stage
+
+        def load_words(src, width, name):
+            t = keep.tile([P, width], I32, name=name, align_bytes=64)
+            nc.sync.dma_start(t[:], src[0].rearrange("p n t -> p (n t)").bitcast(I32))
+            return t
 
         ua_rows = ua.rearrange("(p t) f -> p t f", t=PACK)
         ua_sb = [keep.tile([P, F], F32, name="ua%d" % t) for t in range(PACK)]
-        list2 = load_list(offs2, "list2")
-        ha_sb = load_columns(nc.sync, ha, "ha_sb")
-        xo_sb = keep.tile([P, M], U16, name="xo_sb")
-        nc.sync.dma_start(xo_sb[:].bitcast(I32), xo_words[0].bitcast(I32))
-        nc.sync.dma_start(ua_sb[0][:], ua_rows[:, 0, :])
+        tz_sb = [keep.tile([P, E], F32, name="tz%d" % b) for b in range(NB)]
         xo_stage = keep.tile([P, 2, M // 4], I32, name="xo_stage")
-        for u in range(2):
+        xo_sb = keep.tile([P, M], U16, name="xo_sb")
+
+        def load_xt_scale_rows(q):
             nc.sync.dma_start(
-                xo_stage[64 * u : 64 * u + 4, :, :],
-                xo_scales[0, 8 * u : 8 * u + 8, :].rearrange("(q i) c -> i q c", i=4).bitcast(I32),
+                xt_scale_rows[32 * q + XT_ROW : 32 * q + XT_ROW + 4, :].bitcast(I32),
+                xt_scales[0, 4 * q : 4 * q + 4, :].bitcast(I32),
             )
-        w2_stage = keep.tile([4, QUADS, R // 4], I32, name="w2_stage")
-        nc.sync.dma_start(w2_stage[:], w2_scales[0].rearrange("(q i) c -> i q c", i=4).bitcast(I32))
+
+        nc.sync.dma_start(ua_sb[0][:], ua_rows[:, 0, :])
+        list2 = load_list(offs2, "list2")
+        ha_sb = load_columns(ha, "ha_sb")
+        nc.sync.dma_start(xo_sb[:].bitcast(I32), xo_words[0].bitcast(I32))
         list3 = load_list(offs3, "list3")
+        load_scale_half(xo_stage, xo_scales, 0)
+        load_scale_half(xo_stage, xo_scales, 1)
         nc.sync.dma_start(ua_sb[1][:], ua_rows[:, 1, :])
-        list1 = load_list(offs, "list1")
+        for q in range(3):
+            load_xt_scale_rows(q)
         nc.sync.dma_start(ua_sb[2][:], ua_rows[:, 2, :])
+        load_xt_scale_rows(3)
+        list1 = load_list(offs, "list1")
+        w2_stage = load_scale_whole(w2_scales, R, "w2_stage")
         nc.sync.dma_start(ua_sb[3][:], ua_rows[:, 3, :])
-        w2_sb = keep.tile([P, R], I32, name="w2_sb")
-        nc.sync.dma_start(w2_sb[:], w2_words[0].rearrange("p n t -> p (n t)").bitcast(I32))
-        xt_sb = keep.tile([P, T], I32, name="xt_sb")
-        nc.sync.dma_start(xt_sb[:], xt_words[0].rearrange("p n t -> p (n t)").bitcast(I32))
+        w2_sb = load_words(w2_words, R, "w2_sb")
+        xt_sb = load_words(xt_words, T, "xt_sb")
         list4 = load_list(offs4, "list4")
         list5 = load_list(offs5, "list5")
-        wb_sb = keep.tile([P, N], I32, name="wb_sb", align_bytes=64)
-        nc.sync.dma_start(wb_sb[:], wb_words[0].rearrange("p n t -> p (n t)").bitcast(I32))
-        tz_sb = [keep.tile([P, E], F32, name="tz%d" % b) for b in range(NB)]
+        sa_sb = load_columns(sa, "sa_sb")
+        sb_sb = load_columns(sb, "sb_sb")
+        wb_sb = load_words(wb_words, N, "wb_sb")
         for b in range(NB):
             nc.sync.dma_start(tz_sb[b][:], tz[b * P : (b + 1) * P, :])
+        wb_stage = load_scale_whole(wb_scales, N, "wb_stage")
         list6 = load_list(offs6, "list6")
         list7 = load_list(offs7, "list7")
+        so_sb = load_blocks(so, "so_sb")
+        sp_sb = load_blocks(sp, "sp_sb")
+
+        def spread_halves(rows, stage):
+            words = rows[:].bitcast(I32)
+            for q in range(QUADS):
+                first = 64 * (q // 2)
+                nc.vector.tensor_copy(words[32 * q : 32 * q + 4, :], stage[first : first + 4, q % 2, :])
 
         xo_codes = keep.tile([P, 2 * J], U8, name="xo_codes", align_bytes=64)
         xo_plane = keep.tile([P, J], U8, name="xo_plane", align_bytes=64)
         xt_plane = keep.tile([P, J], U8, name="xt_plane", align_bytes=64)
         nc.vector.tensor_copy(xo_codes[:].bitcast(U16), xo_sb[:].indirect(list3[:]))
-        for q in range(QUADS):
-            first = 64 * (q // 2)
-            nc.vector.tensor_copy(
-                xo_scale_rows[:].bitcast(I32)[32 * q : 32 * q + 4, :], xo_stage[first : first + 4, q % 2, :]
-            )
+        spread_halves(xo_scale_rows, xo_stage)
         nc.vector.tensor_copy(xo_plane[:], xo_scale_rows[:].indirect(list3[:]))
 
         def spread(plane, stage):
@@ -123,19 +137,18 @@ def tile_picked_tokens_codes_bank_pooledgroups_one_lastbounds_kernel(
             for q in range(QUADS):
                 nc.vector.tensor_copy(words[32 * q : 32 * q + 4, :], stage[:, q, :])
 
+        nc.vector.tensor_copy(xt_plane[:], xt_scale_rows[:].indirect(list1[:]))
         spread(w2_scale_rows, w2_stage)
         w2_plane = keep.tile([P, R], U8, name="w2_plane", align_bytes=64)
         nc.vector.tensor_copy(
             w2_plane[:].rearrange("p (m c) -> p m c", m=PACK),
             w2_scale_rows[:].rearrange("p (c m) -> p m c", m=PACK),
         )
-        nc.vector.tensor_copy(xt_plane[:], xt_scale_rows[:].indirect(list1[:]))
-        spread(wb_plane, wb_stage)
 
-        wc_rows = keep.tile([P, PACK, R], BF16, name="wc_rows")
+        wc_rows = [keep.tile([P, 2, R], BF16, name="wc_rows%d" % v) for v in range(2)]
         for t in range(PACK):
             nc.scalar.activation(
-                wc_rows[:, t, :], ua_sb[t][:].indirect(list2[:]), COPY, scale=ha_sb[:, t : t + 1]
+                wc_rows[t // 2][:, t % 2, :], ua_sb[t][:].indirect(list2[:]), COPY, scale=ha_sb[:, t : t + 1]
             )
 
         w2_codes = keep.tile([P, R], I32, name="w2_codes", align_bytes=64)
@@ -160,21 +173,22 @@ def tile_picked_tokens_codes_bank_pooledgroups_one_lastbounds_kernel(
         for m in range(1, PACK):
             notes_pass(a_ps[m - 1][:], m, 0, J)
 
-        wc_view = wc_rows[:].rearrange("p t (g e m) -> p g m e t", e=2, m=PACK)
-        wc_codes, wc_plane = [], []
+        woven = [keep.tile([P, 2 * P * PACK], BF16, name="woven%d" % u, align_bytes=64) for u in range(2)]
+        wc_codes = [keep.tile([P, 2 * P], U32, name="wc_codes%d" % u, align_bytes=64) for u in range(2)]
+        wc_plane = [keep.tile([P, 2 * P], U8, name="wc_plane%d" % u, align_bytes=64) for u in range(2)]
+
+        def weave(u, v):
+            planes = slice(2 * v, 2 * v + 2)
+            nc.vector.tensor_copy(
+                woven[u][:].rearrange("p (m g e t) -> p g m e t", m=2, e=2, t=PACK)[:, :, :, :, planes],
+                wc_rows[v][:].rearrange("p t (g e m) -> p g m e t", e=2, m=PACK)[:, :, 2 * u : 2 * u + 2, :, :],
+            )
+
+        for v in range(2):
+            for u in range(2):
+                weave(u, v)
         for u in range(2):
-            woven = keep.tile([P, 2 * P * PACK], BF16, name="woven%d" % u, align_bytes=64)
-            dst = woven[:].rearrange("p (m g e t) -> p g m e t", m=2, e=2, t=PACK)
-            src = wc_view[:, :, 2 * u : 2 * u + 2, :, :]
-            if u == 0:
-                nc.vector.tensor_copy(dst, src)
-            else:
-                nc.scalar.copy(dst, src)
-            codes = keep.tile([P, 2 * P], U32, name="wc_codes%d" % u, align_bytes=64)
-            plane = keep.tile([P, 2 * P], U8, name="wc_plane%d" % u, align_bytes=64)
-            nc.vector.quantize_mx(out=codes[:].bitcast(FP8X4), scales=plane[:], in_=woven[:])
-            wc_codes.append(codes)
-            wc_plane.append(plane)
+            nc.vector.quantize_mx(out=wc_codes[u][:].bitcast(FP8X4), scales=wc_plane[u][:], in_=woven[u][:])
 
         xt_codes = keep.tile([P, J], U32, name="xt_codes", align_bytes=64)
         for h in range(2):
@@ -199,6 +213,7 @@ def tile_picked_tokens_codes_bank_pooledgroups_one_lastbounds_kernel(
             tokens_pass(a_ps[m - 1][:], m, 0, J)
             nc.vector.tensor_copy(a_sb[m][:], a_ps[m - 1][:])
 
+        spread(wb_plane, wb_stage)
         hid = keep.tile([P, O, PACK], BF16, name="hid", align_bytes=64)
         for m in range(PACK):
             parts = 2 if m == PACK - 1 else 1

@@ -41,7 +41,7 @@ def tile_picked_tokens_codes_bank_pooledgroups_one_lastbounds_kernel(
             return lst
 
         def zeroed_bytes(width, name):
-            t = keep.tile([P, width], U8, name=name, align_bytes=64)
+            t = keep.tile([P, width], U8, name=name, tag=name, align_bytes=64)
             nc.vector.memset(t[:].bitcast(I32), 0)
             return t
 
@@ -83,26 +83,25 @@ def tile_picked_tokens_codes_bank_pooledgroups_one_lastbounds_kernel(
         xo_stage = keep.tile([P, 2, M // 4], I32, name="xo_stage")
         xo_sb = keep.tile([P, M], U16, name="xo_sb")
 
-        def load_xt_scale_rows(q):
+        def load_scale_rows(dst, src, q, first):
             nc.sync.dma_start(
-                xt_scale_rows[32 * q + XT_ROW : 32 * q + XT_ROW + 4, :].bitcast(I32),
-                xt_scales[0, 4 * q : 4 * q + 4, :].bitcast(I32),
+                dst[32 * q + first : 32 * q + first + 4, :].bitcast(I32),
+                src[0, 4 * q : 4 * q + 4, :].bitcast(I32),
             )
 
-        nc.sync.dma_start(ua_sb[0][:], ua_rows[:, 0, :])
-        list2 = load_list(offs2, "list2")
-        ha_sb = load_columns(ha, "ha_sb")
         nc.sync.dma_start(xo_sb[:].bitcast(I32), xo_words[0].bitcast(I32))
         list3 = load_list(offs3, "list3")
         load_scale_half(xo_stage, xo_scales, 0)
         load_scale_half(xo_stage, xo_scales, 1)
+        list2 = load_list(offs2, "list2")
+        ha_sb = load_columns(ha, "ha_sb")
+        nc.sync.dma_start(ua_sb[0][:], ua_rows[:, 0, :])
         nc.sync.dma_start(ua_sb[1][:], ua_rows[:, 1, :])
-        for q in range(3):
-            load_xt_scale_rows(q)
-        nc.sync.dma_start(ua_sb[2][:], ua_rows[:, 2, :])
-        load_xt_scale_rows(3)
+        for q in range(QUADS):
+            load_scale_rows(xt_scale_rows, xt_scales, q, XT_ROW)
         list1 = load_list(offs, "list1")
         w2_stage = load_scale_whole(w2_scales, R, "w2_stage")
+        nc.sync.dma_start(ua_sb[2][:], ua_rows[:, 2, :])
         nc.sync.dma_start(ua_sb[3][:], ua_rows[:, 3, :])
         w2_sb = load_words(w2_words, R, "w2_sb")
         xt_sb = load_words(xt_words, T, "xt_sb")
@@ -113,11 +112,12 @@ def tile_picked_tokens_codes_bank_pooledgroups_one_lastbounds_kernel(
         wb_sb = load_words(wb_words, N, "wb_sb")
         for b in range(NB):
             nc.sync.dma_start(tz_sb[b][:], tz[b * P : (b + 1) * P, :])
-        wb_stage = load_scale_whole(wb_scales, N, "wb_stage")
         list6 = load_list(offs6, "list6")
         list7 = load_list(offs7, "list7")
         so_sb = load_blocks(so, "so_sb")
         sp_sb = load_blocks(sp, "sp_sb")
+        for q in range(QUADS):
+            load_scale_rows(wb_plane, wb_scales, q, 0)
 
         def spread_halves(rows, stage):
             words = rows[:].bitcast(I32)
@@ -173,13 +173,15 @@ def tile_picked_tokens_codes_bank_pooledgroups_one_lastbounds_kernel(
         for m in range(1, PACK):
             notes_pass(a_ps[m - 1][:], m, 0, J)
 
-        woven = [keep.tile([P, 2 * P * PACK], BF16, name="woven%d" % u, align_bytes=64) for u in range(2)]
-        wc_codes = [keep.tile([P, 2 * P], U32, name="wc_codes%d" % u, align_bytes=64) for u in range(2)]
-        wc_plane = [keep.tile([P, 2 * P], U8, name="wc_plane%d" % u, align_bytes=64) for u in range(2)]
+        woven = [
+            keep.tile([P, 2 * P * PACK], BF16, name="woven%d" % u, tag=tag, align_bytes=64)
+            for u, tag in enumerate(("xt_scale_rows", "w2_scale_rows"))
+        ]
 
         def weave(u, v):
             planes = slice(2 * v, 2 * v + 2)
-            nc.vector.tensor_copy(
+            copy = nc.scalar.copy if (u, v) == (1, 1) else nc.vector.tensor_copy
+            copy(
                 woven[u][:].rearrange("p (m g e t) -> p g m e t", m=2, e=2, t=PACK)[:, :, :, :, planes],
                 wc_rows[v][:].rearrange("p t (g e m) -> p g m e t", e=2, m=PACK)[:, :, 2 * u : 2 * u + 2, :, :],
             )
@@ -187,8 +189,14 @@ def tile_picked_tokens_codes_bank_pooledgroups_one_lastbounds_kernel(
         for v in range(2):
             for u in range(2):
                 weave(u, v)
-        for u in range(2):
-            nc.vector.quantize_mx(out=wc_codes[u][:].bitcast(FP8X4), scales=wc_plane[u][:], in_=woven[u][:])
+
+        def quantise_wc(u):
+            codes = keep.tile([P, 2 * P], U32, name="wc_codes", tag="wc_codes", align_bytes=64)
+            plane = keep.tile([P, 2 * P], U8, name="wc_plane", tag="wc_plane", align_bytes=64)
+            nc.vector.quantize_mx(out=codes[:].bitcast(FP8X4), scales=plane[:], in_=woven[u][:])
+            return codes, plane
+
+        wc = quantise_wc(0)
 
         xt_codes = keep.tile([P, J], U32, name="xt_codes", align_bytes=64)
         for h in range(2):
@@ -197,39 +205,42 @@ def tile_picked_tokens_codes_bank_pooledgroups_one_lastbounds_kernel(
                 xt_sb[:].bitcast(U32).indirect(list1[:, h * HALF // 16 : (h + 1) * HALF // 16]),
             )
 
-        def tokens_pass(dst, m, lo, hi):
+        def tokens_pass(dst, wc, m, lo, hi):
             cols = slice(m % 2 * P, (m % 2 + 1) * P)
             nc.tensor.matmul_mx(
-                out=dst, lhsT=wc_codes[m // 2][:, cols].bitcast(FP8X4), lhsT_scale=wc_plane[m // 2][:, cols],
+                out=dst, lhsT=wc[0][:, cols].bitcast(FP8X4), lhsT_scale=wc[1][:, cols],
                 rhs=xt_codes[:, lo:hi].bitcast(FP8X4), rhs_scale=xt_plane[XT_ROW:, lo:hi],
                 start=False, stop=True,
             )
 
         a_sb = [keep.tile([P, J], F32, name="a_sb%d" % m) for m in range(PACK)]
         for h in range(2):
-            tokens_pass(a0_ps[h][:], 0, h * HALF, (h + 1) * HALF)
-            nc.scalar.copy(a_sb[0][:, h * HALF : (h + 1) * HALF], a0_ps[h][:])
-        for m in range(1, PACK):
-            tokens_pass(a_ps[m - 1][:], m, 0, J)
+            tokens_pass(a0_ps[h][:], wc, 0, h * HALF, (h + 1) * HALF)
+            copy = nc.scalar.copy if h == 0 else nc.vector.tensor_copy
+            copy(a_sb[0][:, h * HALF : (h + 1) * HALF], a0_ps[h][:])
+        tokens_pass(a_ps[0][:], wc, 1, 0, J)
+        wc = quantise_wc(1)
+        nc.vector.tensor_copy(a_sb[1][:], a_ps[0][:])
+        for m in range(2, PACK):
+            tokens_pass(a_ps[m - 1][:], wc, m, 0, J)
             nc.vector.tensor_copy(a_sb[m][:], a_ps[m - 1][:])
 
-        spread(wb_plane, wb_stage)
         hid = keep.tile([P, O, PACK], BF16, name="hid", align_bytes=64)
         for m in range(PACK):
             parts = 2 if m == PACK - 1 else 1
             width = S // parts
-            picked = keep.tile([P, parts, 2, width], F32, name="picked", tag="picked", bufs=2)
+            picked = keep.tile([P, 2, S], F32, name="picked", tag="picked", bufs=2)
+            nc.scalar.activation(picked[:, 0, :], a_sb[m][:].indirect(list4[:]), COPY, scale=sa_sb[:, m : m + 1])
             for h in range(parts):
-                cols = slice(h * width // 16, (h + 1) * width // 16)
+                picks = slice(h * width, (h + 1) * width)
                 nc.scalar.activation(
-                    picked[:, h, 0, :], a_sb[m][:].indirect(list4[:, cols]), COPY, scale=sa_sb[:, m : m + 1]
-                )
-                nc.scalar.activation(
-                    picked[:, h, 1, :], a_sb[m][:].indirect(list5[:, cols]), COPY, scale=sb_sb[:, m : m + 1]
+                    picked[:, 1, picks],
+                    a_sb[m][:].indirect(list5[:, h * width // 16 : (h + 1) * width // 16]),
+                    COPY, scale=sb_sb[:, m : m + 1],
                 )
                 nc.vector.tensor_reduce(
                     hid[:, h * width // 2 : (h + 1) * width // 2, m],
-                    picked[:, h, :, :].rearrange("p w (o e) -> p o w e", e=2),
+                    picked[:, :, picks].rearrange("p w (o e) -> p o w e", e=2),
                     XY, MAX,
                 )
 
@@ -260,4 +271,4 @@ def tile_picked_tokens_codes_bank_pooledgroups_one_lastbounds_kernel(
             nc.vector.tensor_tensor(capped[:, b, :], p_ps[:], bounds[:, 0, b, :], MIN)
         for b in range(NB):
             nc.vector.tensor_tensor(result[:, b, :], capped[:, b, :], bounds[:, 1, b, :], MAX)
-        nc.sync.dma_start(out.rearrange("(b p) o -> p b o", p=P), result[:])
+            nc.sync.dma_start(out[b * P : (b + 1) * P, :], result[:, b, :])

@@ -45,8 +45,8 @@ def tile_picked_tokens_codes_bank_pooledgroups_one_lastbounds_kernel(
             nc.vector.memset(t[:].bitcast(I32), 0)
             return t
 
-        xt_scale_rows = zeroed_bytes(T, "xt_scale_rows")
         xo_scale_rows = zeroed_bytes(M, "xo_scale_rows")
+        xt_scale_rows = zeroed_bytes(T, "xt_scale_rows")
         w2_scale_rows = zeroed_bytes(R, "w2_scale_rows")
         wb_plane = zeroed_bytes(N, "wb_plane")
 
@@ -61,12 +61,6 @@ def tile_picked_tokens_codes_bank_pooledgroups_one_lastbounds_kernel(
                 nc.sync.dma_start(t[:], src.rearrange("(b p) o -> p (b o)", p=P))
             return t
 
-        def load_scale_half(stage, src, u):
-            nc.sync.dma_start(
-                stage[64 * u : 64 * u + 4, :, :],
-                src[0, 8 * u : 8 * u + 8, :].rearrange("(q i) c -> i q c", i=4).bitcast(I32),
-            )
-
         def load_scale_whole(src, width, name):
             stage = keep.tile([4, QUADS, width // 4], I32, name=name)
             nc.sync.dma_start(stage[:], src[0].rearrange("(q i) c -> i q c", i=4).bitcast(I32))
@@ -80,28 +74,26 @@ def tile_picked_tokens_codes_bank_pooledgroups_one_lastbounds_kernel(
         ua_rows = ua.rearrange("(p t) f -> p t f", t=PACK)
         ua_sb = [keep.tile([P, F], F32, name="ua%d" % t) for t in range(PACK)]
         tz_sb = [keep.tile([P, E], F32, name="tz%d" % b) for b in range(NB)]
-        xo_stage = keep.tile([P, 2, M // 4], I32, name="xo_stage")
         xo_sb = keep.tile([P, M], U16, name="xo_sb")
 
-        def load_scale_rows(dst, src, q, first):
-            nc.sync.dma_start(
-                dst[32 * q + first : 32 * q + first + 4, :].bitcast(I32),
-                src[0, 4 * q : 4 * q + 4, :].bitcast(I32),
-            )
+        def load_scale_rows(dst, src, i, first):
+            nc.sync.dma_start(dst[first + i : P : 32, :].bitcast(I32), src[0, i : 16 : 4, :].bitcast(I32))
 
         nc.sync.dma_start(xo_sb[:].bitcast(I32), xo_words[0].bitcast(I32))
         list3 = load_list(offs3, "list3")
-        load_scale_half(xo_stage, xo_scales, 0)
-        load_scale_half(xo_stage, xo_scales, 1)
         list2 = load_list(offs2, "list2")
         ha_sb = load_columns(ha, "ha_sb")
-        nc.sync.dma_start(ua_sb[0][:], ua_rows[:, 0, :])
-        nc.sync.dma_start(ua_sb[1][:], ua_rows[:, 1, :])
-        for q in range(QUADS):
-            load_scale_rows(xt_scale_rows, xt_scales, q, XT_ROW)
         list1 = load_list(offs, "list1")
         w2_stage = load_scale_whole(w2_scales, R, "w2_stage")
+        nc.sync.dma_start(ua_sb[0][:], ua_rows[:, 0, :])
+        nc.sync.dma_start(ua_sb[1][:], ua_rows[:, 1, :])
+        for i in range(4):
+            load_scale_rows(xo_scale_rows, xo_scales, i, 0)
+            if i < 2:
+                load_scale_rows(xt_scale_rows, xt_scales, i, XT_ROW)
         nc.sync.dma_start(ua_sb[2][:], ua_rows[:, 2, :])
+        for i in range(2, 4):
+            load_scale_rows(xt_scale_rows, xt_scales, i, XT_ROW)
         nc.sync.dma_start(ua_sb[3][:], ua_rows[:, 3, :])
         w2_sb = load_words(w2_words, R, "w2_sb")
         xt_sb = load_words(xt_words, T, "xt_sb")
@@ -119,17 +111,10 @@ def tile_picked_tokens_codes_bank_pooledgroups_one_lastbounds_kernel(
         for q in range(QUADS):
             load_scale_rows(wb_plane, wb_scales, q, 0)
 
-        def spread_halves(rows, stage):
-            words = rows[:].bitcast(I32)
-            for q in range(QUADS):
-                first = 64 * (q // 2)
-                nc.vector.tensor_copy(words[32 * q : 32 * q + 4, :], stage[first : first + 4, q % 2, :])
-
         xo_codes = keep.tile([P, 2 * J], U8, name="xo_codes", align_bytes=64)
         xo_plane = keep.tile([P, J], U8, name="xo_plane", align_bytes=64)
         xt_plane = keep.tile([P, J], U8, name="xt_plane", align_bytes=64)
         nc.vector.tensor_copy(xo_codes[:].bitcast(U16), xo_sb[:].indirect(list3[:]))
-        spread_halves(xo_scale_rows, xo_stage)
         nc.vector.tensor_copy(xo_plane[:], xo_scale_rows[:].indirect(list3[:]))
 
         def spread(plane, stage):
@@ -175,7 +160,7 @@ def tile_picked_tokens_codes_bank_pooledgroups_one_lastbounds_kernel(
 
         woven = [
             keep.tile([P, 2 * P * PACK], BF16, name="woven%d" % u, tag=tag, align_bytes=64)
-            for u, tag in enumerate(("xt_scale_rows", "w2_scale_rows"))
+            for u, tag in enumerate(("xt_scale_rows", "xo_scale_rows"))
         ]
 
         def weave(u, v):

@@ -15,13 +15,15 @@ MAX = mybir.AluOpType.max
 MIN = mybir.AluOpType.min
 XY = mybir.AxisListType.XY
 
+K, J, R, T, F, Z, M, S, O, N, E = 512, 512, 512, 2048, 2048, 512, 1024, 256, 128, 256, 256
 P = 128
 PACK = 4
 QUADS = 4
-K, J, R, T, F, Z, M, S, O, N, E = 512, 512, 512, 2048, 2048, 512, 1024, 256, 128, 256, 256
+QUAD_ROWS = 4
+ENTRIES = 16
 NB = N // P
-HALF = J // 2
-XT_ROW = 4
+XT_FIRST = 4
+SLOT_RANGES = ((0, 256), (256, 384), (384, 512))
 
 FLOPS = 2 * K * R * J + 2 * Z * R * J + 2 * R * N * O
 
@@ -35,11 +37,6 @@ def tile_picked_tokens_codes_bank_pooledgroups_one_lastbounds_kernel(
         keep = ctx.enter_context(tc.tile_pool(name="keep", bufs=1))
         psum = ctx.enter_context(tc.psum_pool(name="psum", bufs=1))
 
-        def load_list(src, name):
-            lst = keep.tile(list(src.shape), U16, name=name)
-            nc.sync.dma_start(lst[:], src)
-            return lst
-
         def zeroed_bytes(width, name):
             t = keep.tile([P, width], U8, name=name, tag=name, align_bytes=64)
             nc.vector.memset(t[:].bitcast(I32), 0)
@@ -50,80 +47,79 @@ def tile_picked_tokens_codes_bank_pooledgroups_one_lastbounds_kernel(
         w2_scale_rows = zeroed_bytes(R, "w2_scale_rows")
         wb_plane = zeroed_bytes(N, "wb_plane")
 
-        def load_columns(src, name):
+        def load_list(src, name):
+            lst = keep.tile(list(src.shape), U16, name=name)
+            nc.sync.dma_start(lst[:], src)
+            return lst
+
+        def load_dealt_column(src, name):
             t = keep.tile([P, PACK], F32, name=name)
             nc.sync.dma_start(t[:], src.rearrange("(p t) o -> p (t o)", t=PACK))
             return t
 
-        def load_blocks(src, name):
+        def load_block_column(src, name):
             t = keep.tile([P, NB], F32, name=name)
             with nc.allow_non_contiguous_dma(reason="one value a partition and block"):
                 nc.sync.dma_start(t[:], src.rearrange("(b p) o -> p (b o)", p=P))
             return t
-
-        def load_scale_whole(src, width, name):
-            stage = keep.tile([4, QUADS, width // 4], I32, name=name)
-            nc.sync.dma_start(stage[:], src[0].rearrange("(q i) c -> i q c", i=4).bitcast(I32))
-            return stage
 
         def load_words(src, width, name):
             t = keep.tile([P, width], I32, name=name, align_bytes=64)
             nc.sync.dma_start(t[:], src[0].rearrange("p n t -> p (n t)").bitcast(I32))
             return t
 
+        def load_scale_rows(dst, src, i, first):
+            nc.sync.dma_start(
+                dst[first + i : P : 32, :].bitcast(I32), src[0, i : QUADS * QUAD_ROWS : QUAD_ROWS, :].bitcast(I32)
+            )
+
         ua_rows = ua.rearrange("(p t) f -> p t f", t=PACK)
         ua_sb = [keep.tile([P, F], F32, name="ua%d" % t) for t in range(PACK)]
         tz_sb = [keep.tile([P, E], F32, name="tz%d" % b) for b in range(NB)]
         xo_sb = keep.tile([P, M], U16, name="xo_sb")
 
-        def load_scale_rows(dst, src, i, first):
-            nc.sync.dma_start(dst[first + i : P : 32, :].bitcast(I32), src[0, i : 16 : 4, :].bitcast(I32))
-
         nc.sync.dma_start(xo_sb[:].bitcast(I32), xo_words[0].bitcast(I32))
         list3 = load_list(offs3, "list3")
         list2 = load_list(offs2, "list2")
-        ha_sb = load_columns(ha, "ha_sb")
+        ha_sb = load_dealt_column(ha, "ha_sb")
         list1 = load_list(offs, "list1")
-        w2_stage = load_scale_whole(w2_scales, R, "w2_stage")
+        w2_stage = keep.tile([QUAD_ROWS, QUADS, R // 4], I32, name="w2_stage")
+        nc.sync.dma_start(w2_stage[:], w2_scales[0].rearrange("(q i) c -> i q c", i=QUAD_ROWS).bitcast(I32))
         nc.sync.dma_start(ua_sb[0][:], ua_rows[:, 0, :])
         nc.sync.dma_start(ua_sb[1][:], ua_rows[:, 1, :])
-        for i in range(4):
+        for i in range(QUAD_ROWS):
             load_scale_rows(xo_scale_rows, xo_scales, i, 0)
-            if i < 2:
-                load_scale_rows(xt_scale_rows, xt_scales, i, XT_ROW)
+            if i < QUAD_ROWS // 2:
+                load_scale_rows(xt_scale_rows, xt_scales, i, XT_FIRST)
         nc.sync.dma_start(ua_sb[2][:], ua_rows[:, 2, :])
-        for i in range(2, 4):
-            load_scale_rows(xt_scale_rows, xt_scales, i, XT_ROW)
+        for i in range(QUAD_ROWS // 2, QUAD_ROWS):
+            load_scale_rows(xt_scale_rows, xt_scales, i, XT_FIRST)
         nc.sync.dma_start(ua_sb[3][:], ua_rows[:, 3, :])
         w2_sb = load_words(w2_words, R, "w2_sb")
         xt_sb = load_words(xt_words, T, "xt_sb")
         list4 = load_list(offs4, "list4")
         list5 = load_list(offs5, "list5")
-        sa_sb = load_columns(sa, "sa_sb")
-        sb_sb = load_columns(sb, "sb_sb")
+        sa_sb = load_dealt_column(sa, "sa_sb")
+        sb_sb = load_dealt_column(sb, "sb_sb")
         wb_sb = load_words(wb_words, N, "wb_sb")
         for b in range(NB):
             nc.sync.dma_start(tz_sb[b][:], tz[b * P : (b + 1) * P, :])
         list6 = load_list(offs6, "list6")
         list7 = load_list(offs7, "list7")
-        so_sb = load_blocks(so, "so_sb")
-        sp_sb = load_blocks(sp, "sp_sb")
-        for q in range(QUADS):
-            load_scale_rows(wb_plane, wb_scales, q, 0)
+        so_sb = load_block_column(so, "so_sb")
+        sp_sb = load_block_column(sp, "sp_sb")
+        for i in range(QUAD_ROWS):
+            load_scale_rows(wb_plane, wb_scales, i, 0)
 
         xo_codes = keep.tile([P, 2 * J], U8, name="xo_codes", align_bytes=64)
         xo_plane = keep.tile([P, J], U8, name="xo_plane", align_bytes=64)
         xt_plane = keep.tile([P, J], U8, name="xt_plane", align_bytes=64)
         nc.vector.tensor_copy(xo_codes[:].bitcast(U16), xo_sb[:].indirect(list3[:]))
         nc.vector.tensor_copy(xo_plane[:], xo_scale_rows[:].indirect(list3[:]))
-
-        def spread(plane, stage):
-            words = plane[:].bitcast(I32)
-            for q in range(QUADS):
-                nc.vector.tensor_copy(words[32 * q : 32 * q + 4, :], stage[:, q, :])
-
         nc.vector.tensor_copy(xt_plane[:], xt_scale_rows[:].indirect(list1[:]))
-        spread(w2_scale_rows, w2_stage)
+
+        for q in range(QUADS):
+            nc.vector.tensor_copy(w2_scale_rows[:].bitcast(I32)[32 * q : 32 * q + QUAD_ROWS, :], w2_stage[:, q, :])
         w2_plane = keep.tile([P, R], U8, name="w2_plane", align_bytes=64)
         nc.vector.tensor_copy(
             w2_plane[:].rearrange("p (m c) -> p m c", m=PACK),
@@ -142,8 +138,8 @@ def tile_picked_tokens_codes_bank_pooledgroups_one_lastbounds_kernel(
             w2_sb[:].rearrange("p (g e m) -> p g m e", m=PACK, e=4),
         )
 
-        a0_ps = [psum.tile([P, HALF], F32, name="a0_ps%d" % h) for h in range(2)]
-        a_ps = [psum.tile([P, J], F32, name="a_ps%d" % m) for m in range(1, PACK)]
+        a0_ps = [psum.tile([P, hi - lo], F32, name="a0_ps%d" % lo) for lo, hi in SLOT_RANGES]
+        a_ps = {m: psum.tile([P, J], F32, name="a_ps%d" % m) for m in range(1, PACK)}
 
         def notes_pass(dst, m, lo, hi):
             cols = slice(m * P, (m + 1) * P)
@@ -153,27 +149,22 @@ def tile_picked_tokens_codes_bank_pooledgroups_one_lastbounds_kernel(
                 start=True, stop=False,
             )
 
-        for h in range(2):
-            notes_pass(a0_ps[h][:], 0, h * HALF, (h + 1) * HALF)
+        for bank, (lo, hi) in zip(a0_ps, SLOT_RANGES):
+            notes_pass(bank[:], 0, lo, hi)
         for m in range(1, PACK):
-            notes_pass(a_ps[m - 1][:], m, 0, J)
+            notes_pass(a_ps[m][:], m, 0, J)
 
         woven = [
             keep.tile([P, 2 * P * PACK], BF16, name="woven%d" % u, tag=tag, align_bytes=64)
             for u, tag in enumerate(("xt_scale_rows", "xo_scale_rows"))
         ]
-
-        def weave(u, v):
-            planes = slice(2 * v, 2 * v + 2)
-            copy = nc.scalar.copy if (u, v) == (1, 1) else nc.vector.tensor_copy
-            copy(
-                woven[u][:].rearrange("p (m g e t) -> p g m e t", m=2, e=2, t=PACK)[:, :, :, :, planes],
-                wc_rows[v][:].rearrange("p t (g e m) -> p g m e t", e=2, m=PACK)[:, :, 2 * u : 2 * u + 2, :, :],
-            )
-
         for v in range(2):
             for u in range(2):
-                weave(u, v)
+                copy = nc.scalar.copy if (u, v) == (1, 1) else nc.vector.tensor_copy
+                copy(
+                    woven[u][:].rearrange("p (m g e t) -> p g m e t", m=2, e=2, t=PACK)[:, :, :, :, 2 * v : 2 * v + 2],
+                    wc_rows[v][:].rearrange("p t (g e m) -> p g m e t", e=2, m=PACK)[:, :, 2 * u : 2 * u + 2, :, :],
+                )
 
         def quantise_wc(u):
             codes = keep.tile([P, 2 * P], U32, name="wc_codes", tag="wc_codes", align_bytes=64)
@@ -181,46 +172,46 @@ def tile_picked_tokens_codes_bank_pooledgroups_one_lastbounds_kernel(
             nc.vector.quantize_mx(out=codes[:].bitcast(FP8X4), scales=plane[:], in_=woven[u][:])
             return codes, plane
 
-        wc = quantise_wc(0)
+        wc_low = quantise_wc(0)
 
         xt_codes = keep.tile([P, J], U32, name="xt_codes", align_bytes=64)
-        for h in range(2):
+        for lo, hi in SLOT_RANGES:
             nc.vector.tensor_copy(
-                xt_codes[:, h * HALF : (h + 1) * HALF],
-                xt_sb[:].bitcast(U32).indirect(list1[:, h * HALF // 16 : (h + 1) * HALF // 16]),
+                xt_codes[:, lo:hi], xt_sb[:].bitcast(U32).indirect(list1[:, lo // ENTRIES : hi // ENTRIES])
             )
 
         def tokens_pass(dst, wc, m, lo, hi):
+            codes, plane = wc
             cols = slice(m % 2 * P, (m % 2 + 1) * P)
             nc.tensor.matmul_mx(
-                out=dst, lhsT=wc[0][:, cols].bitcast(FP8X4), lhsT_scale=wc[1][:, cols],
-                rhs=xt_codes[:, lo:hi].bitcast(FP8X4), rhs_scale=xt_plane[XT_ROW:, lo:hi],
+                out=dst, lhsT=codes[:, cols].bitcast(FP8X4), lhsT_scale=plane[:, cols],
+                rhs=xt_codes[:, lo:hi].bitcast(FP8X4), rhs_scale=xt_plane[XT_FIRST:, lo:hi],
                 start=False, stop=True,
             )
 
         a_sb = [keep.tile([P, J], F32, name="a_sb%d" % m) for m in range(PACK)]
-        for h in range(2):
-            tokens_pass(a0_ps[h][:], wc, 0, h * HALF, (h + 1) * HALF)
-            copy = nc.scalar.copy if h == 0 else nc.vector.tensor_copy
-            copy(a_sb[0][:, h * HALF : (h + 1) * HALF], a0_ps[h][:])
-        tokens_pass(a_ps[0][:], wc, 1, 0, J)
-        wc = quantise_wc(1)
-        nc.vector.tensor_copy(a_sb[1][:], a_ps[0][:])
+        for bank, (lo, hi) in zip(a0_ps, SLOT_RANGES):
+            tokens_pass(bank[:], wc_low, 0, lo, hi)
+            copy = nc.vector.tensor_copy if hi == J else nc.scalar.copy
+            copy(a_sb[0][:, lo:hi], bank[:])
+        tokens_pass(a_ps[1][:], wc_low, 1, 0, J)
+        nc.vector.tensor_copy(a_sb[1][:], a_ps[1][:])
+        wc_high = quantise_wc(1)
         for m in range(2, PACK):
-            tokens_pass(a_ps[m - 1][:], wc, m, 0, J)
-            nc.vector.tensor_copy(a_sb[m][:], a_ps[m - 1][:])
+            tokens_pass(a_ps[m][:], wc_high, m, 0, J)
+            nc.vector.tensor_copy(a_sb[m][:], a_ps[m][:])
 
-        hid = keep.tile([P, O, PACK], BF16, name="hid", align_bytes=64)
+        hid = keep.tile([P, O, PACK], BF16, name="hid", tag="wc_codes", align_bytes=64)
         for m in range(PACK):
             parts = 2 if m == PACK - 1 else 1
             width = S // parts
-            picked = keep.tile([P, 2, S], F32, name="picked", tag="picked", bufs=2)
+            picked = keep.tile([P, 2, S], F32, name="picked%d" % m, tag="picked%d" % m)
             nc.scalar.activation(picked[:, 0, :], a_sb[m][:].indirect(list4[:]), COPY, scale=sa_sb[:, m : m + 1])
             for h in range(parts):
                 picks = slice(h * width, (h + 1) * width)
                 nc.scalar.activation(
                     picked[:, 1, picks],
-                    a_sb[m][:].indirect(list5[:, h * width // 16 : (h + 1) * width // 16]),
+                    a_sb[m][:].indirect(list5[:, h * width // ENTRIES : (h + 1) * width // ENTRIES]),
                     COPY, scale=sb_sb[:, m : m + 1],
                 )
                 nc.vector.tensor_reduce(
@@ -229,15 +220,12 @@ def tile_picked_tokens_codes_bank_pooledgroups_one_lastbounds_kernel(
                     XY, MAX,
                 )
 
-        bounds = keep.tile([P, 2, NB, O], F32, name="bounds", tag="picked", bufs=2)
-        for b in range(NB):
-            nc.scalar.activation(
-                bounds[:, 0, b, :], tz_sb[b][:].indirect(list6[:]), COPY, scale=so_sb[:, b : b + 1]
-            )
-        for b in range(NB):
-            nc.scalar.activation(
-                bounds[:, 1, b, :], tz_sb[b][:].indirect(list7[:]), COPY, scale=sp_sb[:, b : b + 1]
-            )
+        bounds = keep.tile([P, 2, NB, O], F32, name="bounds", tag="picked%d" % (PACK - 2))
+        for side, (lst, step) in enumerate(((list6, so_sb), (list7, sp_sb))):
+            for b in range(NB):
+                nc.scalar.activation(
+                    bounds[:, side, b, :], tz_sb[b][:].indirect(lst[:]), COPY, scale=step[:, b : b + 1]
+                )
 
         hid_codes = keep.tile([P, O], U32, name="hid_codes", align_bytes=64)
         hid_plane = keep.tile([P, O], U8, name="hid_plane", align_bytes=64)

from contextlib import ExitStack

import concourse.mybir as mybir

F32 = mybir.dt.float32
BF16 = mybir.dt.bfloat16
I32 = mybir.dt.int32
U32 = mybir.dt.uint32
U16 = mybir.dt.uint16
U8 = mybir.dt.uint8
FP8X4 = mybir.dt.float8_e4m3fn_x4
FP4X4 = mybir.dt.float4_e2m1fn_x4
COPY = mybir.ActivationFunctionType.Copy
MAX = mybir.AluOpType.max
MIN = mybir.AluOpType.min
XY = mybir.AxisListType.XY

K, J, R, T, F, Z, M, S, O, N, E = 512, 512, 512, 2048, 2048, 512, 1024, 256, 128, 256, 256
P = 128
PACK = 4
QUADS = 4
QUAD_ROWS = 4
ENTRIES = 16
NB = N // P
XT_FIRST = 4
SLOT_RANGES = ((0, 256), (256, 384), (384, 512))

FLOPS = 2 * K * R * J + 2 * Z * R * J + 2 * R * N * O


def tile_picked_tokens_codes_bank_pooledgroups_one_lastbounds_kernel(
    tc, xt_words, xt_scales, ua, ha, xo_words, xo_scales, w2_words, w2_scales, sa, sb,
    wb_words, wb_scales, tz, so, sp, offs, offs2, offs3, offs4, offs5, offs6, offs7, out,
):
    nc = tc.nc
    with ExitStack() as ctx:
        keep = ctx.enter_context(tc.tile_pool(name="keep", bufs=1))
        psum = ctx.enter_context(tc.psum_pool(name="psum", bufs=1))

        def zeroed_bytes(width, name):
            t = keep.tile([P, width], U8, name=name, tag=name, align_bytes=64)
            nc.vector.memset(t[:].bitcast(I32), 0)
            return t

        xo_scale_rows = zeroed_bytes(M, "xo_scale_rows")
        xt_scale_rows = zeroed_bytes(T, "xt_scale_rows")
        w2_scale_rows = zeroed_bytes(R, "w2_scale_rows")
        wb_plane = zeroed_bytes(N, "wb_plane")

        def load_list(src, name):
            lst = keep.tile(list(src.shape), U16, name=name)
            nc.sync.dma_start(lst[:], src)
            return lst

        def load_dealt_column(src, name):
            t = keep.tile([P, PACK], F32, name=name)
            nc.sync.dma_start(t[:], src.rearrange("(p t) o -> p (t o)", t=PACK))
            return t

        def load_block_column(src, name):
            t = keep.tile([P, NB], F32, name=name)
            with nc.allow_non_contiguous_dma(reason="one value a partition and block"):
                nc.sync.dma_start(t[:], src.rearrange("(b p) o -> p (b o)", p=P))
            return t

        def load_words(src, width, name):
            t = keep.tile([P, width], I32, name=name, align_bytes=64)
            nc.sync.dma_start(t[:], src[0].rearrange("p n t -> p (n t)").bitcast(I32))
            return t

        def load_scale_rows(dst, src, i, first):
            nc.sync.dma_start(
                dst[first + i : P : 32, :].bitcast(I32), src[0, i : QUADS * QUAD_ROWS : QUAD_ROWS, :].bitcast(I32)
            )

        ua_rows = ua.rearrange("(p t) f -> p t f", t=PACK)
        ua_sb = [keep.tile([P, F], F32, name="ua%d" % t) for t in range(PACK)]
        tz_sb = [keep.tile([P, E], F32, name="tz%d" % b) for b in range(NB)]
        xo_sb = keep.tile([P, M], U16, name="xo_sb")

        nc.sync.dma_start(xo_sb[:].bitcast(I32), xo_words[0].bitcast(I32))
        list3 = load_list(offs3, "list3")
        list2 = load_list(offs2, "list2")
        ha_sb = load_dealt_column(ha, "ha_sb")
        list1 = load_list(offs, "list1")
        w2_stage = keep.tile([QUAD_ROWS, QUADS, R // 4], I32, name="w2_stage")
        nc.sync.dma_start(w2_stage[:], w2_scales[0].rearrange("(q i) c -> i q c", i=QUAD_ROWS).bitcast(I32))
        nc.sync.dma_start(ua_sb[0][:], ua_rows[:, 0, :])
        nc.sync.dma_start(ua_sb[1][:], ua_rows[:, 1, :])
        for i in range(QUAD_ROWS):
            load_scale_rows(xo_scale_rows, xo_scales, i, 0)
            if i < QUAD_ROWS // 2:
                load_scale_rows(xt_scale_rows, xt_scales, i, XT_FIRST)
        nc.sync.dma_start(ua_sb[2][:], ua_rows[:, 2, :])
        for i in range(QUAD_ROWS // 2, QUAD_ROWS):
            load_scale_rows(xt_scale_rows, xt_scales, i, XT_FIRST)
        nc.sync.dma_start(ua_sb[3][:], ua_rows[:, 3, :])
        w2_sb = load_words(w2_words, R, "w2_sb")
        xt_sb = load_words(xt_words, T, "xt_sb")
        list4 = load_list(offs4, "list4")
        list5 = load_list(offs5, "list5")
        sa_sb = load_dealt_column(sa, "sa_sb")
        sb_sb = load_dealt_column(sb, "sb_sb")
        wb_sb = load_words(wb_words, N, "wb_sb")
        for b in range(NB):
            nc.sync.dma_start(tz_sb[b][:], tz[b * P : (b + 1) * P, :])
        list6 = load_list(offs6, "list6")
        list7 = load_list(offs7, "list7")
        so_sb = load_block_column(so, "so_sb")
        sp_sb = load_block_column(sp, "sp_sb")
        for i in range(QUAD_ROWS):
            load_scale_rows(wb_plane, wb_scales, i, 0)

        xo_codes = keep.tile([P, 2 * J], U8, name="xo_codes", align_bytes=64)
        xo_plane = keep.tile([P, J], U8, name="xo_plane", align_bytes=64)
        xt_plane = keep.tile([P, J], U8, name="xt_plane", align_bytes=64)
        nc.vector.tensor_copy(xo_codes[:].bitcast(U16), xo_sb[:].indirect(list3[:]))
        nc.vector.tensor_copy(xo_plane[:], xo_scale_rows[:].indirect(list3[:]))
        nc.vector.tensor_copy(xt_plane[:], xt_scale_rows[:].indirect(list1[:]))

        for q in range(QUADS):
            nc.vector.tensor_copy(w2_scale_rows[:].bitcast(I32)[32 * q : 32 * q + QUAD_ROWS, :], w2_stage[:, q, :])
        w2_plane = keep.tile([P, R], U8, name="w2_plane", align_bytes=64)
        nc.vector.tensor_copy(
            w2_plane[:].rearrange("p (m c) -> p m c", m=PACK),
            w2_scale_rows[:].rearrange("p (c m) -> p m c", m=PACK),
        )

        wc_rows = [keep.tile([P, 2, R], BF16, name="wc_rows%d" % v) for v in range(2)]
        for t in range(PACK):
            nc.scalar.activation(
                wc_rows[t // 2][:, t % 2, :], ua_sb[t][:].indirect(list2[:]), COPY, scale=ha_sb[:, t : t + 1]
            )

        w2_codes = keep.tile([P, R], I32, name="w2_codes", align_bytes=64)
        nc.vector.tensor_copy(
            w2_codes[:].rearrange("p (m g e) -> p g m e", m=PACK, e=4),
            w2_sb[:].rearrange("p (g e m) -> p g m e", m=PACK, e=4),
        )

        a0_ps = [psum.tile([P, hi - lo], F32, name="a0_ps%d" % lo) for lo, hi in SLOT_RANGES]
        a_ps = {m: psum.tile([P, J], F32, name="a_ps%d" % m) for m in range(1, PACK)}

        def notes_pass(dst, m, lo, hi):
            cols = slice(m * P, (m + 1) * P)
            nc.tensor.matmul_mx(
                out=dst, lhsT=w2_codes[:, cols].bitcast(FP8X4), lhsT_scale=w2_plane[:, cols],
                rhs=xo_codes[:, 2 * lo : 2 * hi].bitcast(FP4X4), rhs_scale=xo_plane[:, lo:hi],
                start=True, stop=False,
            )

        for bank, (lo, hi) in zip(a0_ps, SLOT_RANGES):
            notes_pass(bank[:], 0, lo, hi)
        for m in range(1, PACK):
            notes_pass(a_ps[m][:], m, 0, J)

        woven = [
            keep.tile([P, 2 * P * PACK], BF16, name="woven%d" % u, tag=tag, align_bytes=64)
            for u, tag in enumerate(("xt_scale_rows", "xo_scale_rows"))
        ]
        for v in range(2):
            for u in range(2):
                copy = nc.scalar.copy if (u, v) == (1, 1) else nc.vector.tensor_copy
                copy(
                    woven[u][:].rearrange("p (m g e t) -> p g m e t", m=2, e=2, t=PACK)[:, :, :, :, 2 * v : 2 * v + 2],
                    wc_rows[v][:].rearrange("p t (g e m) -> p g m e t", e=2, m=PACK)[:, :, 2 * u : 2 * u + 2, :, :],
                )

        def quantise_wc(u):
            codes = keep.tile([P, 2 * P], U32, name="wc_codes", tag="wc_codes", align_bytes=64)
            plane = keep.tile([P, 2 * P], U8, name="wc_plane", tag="wc_plane", align_bytes=64)
            nc.vector.quantize_mx(out=codes[:].bitcast(FP8X4), scales=plane[:], in_=woven[u][:])
            return codes, plane

        wc_low = quantise_wc(0)

        xt_codes = keep.tile([P, J], U32, name="xt_codes", align_bytes=64)
        for lo, hi in SLOT_RANGES:
            nc.vector.tensor_copy(
                xt_codes[:, lo:hi], xt_sb[:].bitcast(U32).indirect(list1[:, lo // ENTRIES : hi // ENTRIES])
            )

        def tokens_pass(dst, wc, m, lo, hi):
            codes, plane = wc
            cols = slice(m % 2 * P, (m % 2 + 1) * P)
            nc.tensor.matmul_mx(
                out=dst, lhsT=codes[:, cols].bitcast(FP8X4), lhsT_scale=plane[:, cols],
                rhs=xt_codes[:, lo:hi].bitcast(FP8X4), rhs_scale=xt_plane[XT_FIRST:, lo:hi],
                start=False, stop=True,
            )

        a_sb = [keep.tile([P, J], F32, name="a_sb%d" % m) for m in range(PACK)]
        for bank, (lo, hi) in zip(a0_ps, SLOT_RANGES):
            tokens_pass(bank[:], wc_low, 0, lo, hi)
            copy = nc.vector.tensor_copy if hi == J else nc.scalar.copy
            copy(a_sb[0][:, lo:hi], bank[:])
        tokens_pass(a_ps[1][:], wc_low, 1, 0, J)
        nc.vector.tensor_copy(a_sb[1][:], a_ps[1][:])
        wc_high = quantise_wc(1)
        for m in range(2, PACK):
            tokens_pass(a_ps[m][:], wc_high, m, 0, J)
            nc.vector.tensor_copy(a_sb[m][:], a_ps[m][:])

        hid = keep.tile([P, O, PACK], BF16, name="hid", tag="wc_codes", align_bytes=64)
        for m in range(PACK):
            parts = 2 if m == PACK - 1 else 1
            width = S // parts
            picked = keep.tile([P, 2, S], F32, name="picked%d" % m, tag="picked%d" % m)
            nc.scalar.activation(picked[:, 0, :], a_sb[m][:].indirect(list4[:]), COPY, scale=sa_sb[:, m : m + 1])
            for h in range(parts):
                picks = slice(h * width, (h + 1) * width)
                nc.scalar.activation(
                    picked[:, 1, picks],
                    a_sb[m][:].indirect(list5[:, h * width // ENTRIES : (h + 1) * width // ENTRIES]),
                    COPY, scale=sb_sb[:, m : m + 1],
                )
                nc.vector.tensor_reduce(
                    hid[:, h * width // 2 : (h + 1) * width // 2, m],
                    picked[:, :, picks].rearrange("p w (o e) -> p o w e", e=2),
                    XY, MAX,
                )

        bounds = keep.tile([P, 2, NB, O], F32, name="bounds", tag="picked%d" % (PACK - 2))
        for side, (lst, step) in enumerate(((list6, so_sb), (list7, sp_sb))):
            for b in range(NB):
                nc.scalar.activation(
                    bounds[:, side, b, :], tz_sb[b][:].indirect(lst[:]), COPY, scale=step[:, b : b + 1]
                )

        hid_codes = keep.tile([P, O], U32, name="hid_codes", align_bytes=64)
        hid_plane = keep.tile([P, O], U8, name="hid_plane", align_bytes=64)
        nc.vector.quantize_mx(
            out=hid_codes[:].bitcast(FP8X4), scales=hid_plane[:], in_=hid[:].rearrange("p o m -> p (o m)")
        )
        capped = keep.tile([P, NB, O], F32, name="capped")
        result = keep.tile([P, NB, O], F32, name="result")
        for b in range(NB):
            cols = slice(b * P, (b + 1) * P)
            p_ps = psum.tile([P, O], F32, name="p_ps%d" % b)
            nc.tensor.matmul_mx(
                out=p_ps[:], lhsT=wb_sb[:, cols].bitcast(FP8X4), lhsT_scale=wb_plane[:, cols],
                rhs=hid_codes[:].bitcast(FP8X4), rhs_scale=hid_plane[:], start=True, stop=True,
            )
            nc.vector.tensor_tensor(capped[:, b, :], p_ps[:], bounds[:, 0, b, :], MIN)
        for b in range(NB):
            nc.vector.tensor_tensor(result[:, b, :], capped[:, b, :], bounds[:, 1, b, :], MAX)
            nc.sync.dma_start(out[b * P : (b + 1) * P, :], result[:, b, :])
